import numpy as np, ml_dtypes
CORES = [83,85,87,115,117,119]
N = 6
BF = ml_dtypes.bfloat16
W, L, S, T, F = 4096, 192, 1, 6, 64
C = W >> S
LEVELS = np.array([800, 900, 1000, 1050, 1100, 1150, 1250, 1400])
def parts(rng):
    d = {"key": rng.integers(0, 256, (N, 8, 16, W)), "em": rng.integers(0, 256, (N, 8, 16, W)), "cl": rng.integers(0, W, (N, 8, 16, C)), "pl": rng.integers(0, W, (N, 8, 16, L)),
         "q": rng.integers(0, 256, (N, 8, 16, L)), "emb": rng.integers(0, 256, (N, 8, 16, 16)), "w": rng.integers(0, 256, (N, 8, 16, 1))}
    base = np.stack([rng.permutation(LEVELS) for r in range(N)]).reshape(N, 8, 1, 1)
    d["th"] = base + rng.integers(-100, 101, (N, 8, 16, 1))
    return d
def pack(d):
    kinds = {"key": BF, "em": BF, "cl": np.int32, "pl": np.int32, "q": BF, "emb": BF, "w": BF, "th": np.float32}
    return {k: np.ascontiguousarray(d[k].reshape(N, 128, -1)).astype(np.float32).astype(t) for k, t in kinds.items()}
def setup_inputs(rng):
    return pack(parts(rng))
def setup_inputs_ties(rng):
    d = parts(rng); o = rng.permutation(8)
    for k in ("key", "q", "emb"): d[k] = 64 * rng.integers(0, 4, d[k].shape)
    d["th"] = 64 * rng.integers(16, 23, (N, 8, 16, 1)) + rng.integers(0, 2, (N, 8, 16, 1))
    d["em"] = rng.integers(0, 2, (N, 8, 16, W)) * rng.choice(np.array([1, 3, 255]), (N, 8, 1, 1))
    d["em"][:, o[0]] = 7; d["em"][:, o[1]] = 0
    for k in ("key", "q", "emb"):
        d[k][:, o[2]] = 0
        d[k][:, o[3]] = rng.integers(0, 32, d[k][:, o[3]].shape)
    d["th"][:, o[2], :, 0] = rng.permutation(np.arange(16) % 3)
    d["th"][:, o[3]] = rng.integers(1, 256, (N, 16, 1))
    return pack(d)
def setup_inputs_ends(rng):
    d = parts(rng); o = rng.permutation(8); ends = np.array([0, 1, W - 2, W - 1])
    d["pl"][:, o[0]] = rng.choice(ends, (N, 16, L)); d["th"][:, o[0]] = 4096
    d["th"][:, o[1]] = 0
    d["pl"][:, o[2]] = rng.integers(0, W, (N, 1, L))
    d["cl"][:, o[3]] = rng.choice(ends, (N, 16, C)); d["th"][:, o[3]] = 1000
    d["cl"][:, o[4]] = rng.integers(0, W, (N, 1, C))
    d["key"][:, o[5]] = d["key"][:, o[5]][:, :, :1]
    d["pl"][:, o[6]] = rng.choice(ends, (N, 16, L))
    d["th"][:, o[7]] = 0; d["w"][:, o[7]] = 0
    return pack(d)
def setup_inputs_lone(rng):
    d = parts(rng); d["th"] = np.zeros((N, 8, 16, 1), np.int64)
    for r in range(N):
        o = rng.permutation(8)
        d["th"][r, o[1], 0] = 4096; d["th"][r, o[2], 15] = 4096; d["th"][r, o[3], 14:] = 4096
        for g in o[4:]: d["th"][r, g, rng.integers(1, 15)] = 4096
    d["th"][rng.integers(0, N)] = 0
    return pack(d)
def setup_inputs_big(rng):
    d = parts(rng); o = rng.permutation(8)
    for k in ("key", "em", "q", "emb"): d[k] = 255 * rng.integers(0, 2, d[k].shape)
    d["w"] = rng.integers(254, 256, d["w"].shape)
    d["th"] = rng.choice(np.array([1785, 1786, 2040, 2041, 2295, 1020, 4080, 4081]), (N, 8, 16, 1))
    d["key"][:, o[0]] = 0; d["q"][:, o[0]] = 255; d["emb"][:, o[0]] = 255; d["w"][:, o[0]] = 255
    d["th"][:, o[0], :, 0] = 4080 + np.arange(16) % 2
    d["em"][:, o[1]] = 255
    d["th"][:, o[2]] = 0
    d["th"][:, o[3]] = 0; d["q"][:, o[3]] = 255; d["emb"][:, o[3]] = 255; d["w"][:, o[3]] = 255
    d["em"][:, o[4]] = 255 - (rng.random((N, 16, W)) < 0.0625)
    return pack(d)
def setup_inputs_spread(rng):
    d = parts(rng)
    for k in ("key", "em", "q", "emb"):
        s = d[k].shape
        d[k] = np.minimum((np.exp2(10 * rng.random(s[:2] + (1, s[3]))) * rng.random(s)).astype(np.int64), 255)
    d["w"] = np.minimum(np.exp2(8 * rng.random(d["w"].shape)).astype(np.int64), 255)
    d["th"] = np.minimum(np.exp2(8 + 4 * rng.random((N, 8, 16, 1))).astype(np.int64), 4096)
    for k in ("pl", "cl"): d[k] = np.minimum((W * rng.random(d[k].shape) ** 3).astype(np.int64), W - 1)
    return pack(d)
def check_inputs(d):
    bad = []
    for k, hi in (("key", 255), ("em", 255), ("cl", W - 1), ("pl", W - 1), ("q", 255), ("emb", 255), ("w", 255), ("th", 4096)):
        a = np.asarray(d[k]).astype(np.float64)
        if not np.all((a >= 0) & (a <= hi) & (a == np.floor(a))): bad.append("whole numbers and range of " + k)
    return bad
def reference(key, em, cl, pl, q, emb, w, th):
    def ints(a): return a.astype(np.float32).astype(np.int32).reshape(N, 8, 16, -1)
    K, E, CL, B, H, TH = ints(key), ints(em), ints(cl), ints(emb), ints(w), ints(th)
    p, x = ints(pl), ints(q)
    toks = [[] for r in range(N)]
    for t in range(T):
        pn, xn = [], []
        for r in range(N):
            at = np.take_along_axis(K[r], p[r].reshape(8, 1, 16 * L), 2).reshape(8, 16, 16, L)
            dist = np.add.reduce(np.abs(at - x[r][:, :, None, :]), axis=1)
            near = dist < TH[r]
            first = np.argmax(near, axis=1)
            lead = np.take_along_axis(p[r], first[:, None, :], 1)[:, 0]
            h = np.add.reduce(H[r] * x[r], axis=1)
            c = np.where(np.any(near, axis=1), lead >> S, h & (C - 1))
            pr = np.where(near, p[r], np.take_along_axis(CL[r], c[:, None, :], 2))
            v = np.add.reduce(np.take_along_axis(E[r], pr.reshape(8, 1, 16 * L), 2).reshape(8, 16, 16, L), axis=2)
            tok = np.argmax(v, axis=1)
            toks[r].append(tok)
            xn.append((x[r] + np.take_along_axis(B[r], tok[:, :, None], 1).transpose(0, 2, 1)) >> 1); pn.append(pr)
        p = np.stack([np.concatenate([(pn[(r - 1) % N][..., :F] + (1 if r == 0 else 0)) & (W - 1), (pn[(r + 1) % N][..., F:] - (1 if r == N - 1 else 0)) & (W - 1)], axis=2) for r in range(N)])
        x = np.stack([np.concatenate([xn[(r - 1) % N][..., :F], xn[(r + 1) % N][..., F:]], axis=2) for r in range(N)])
    yt = np.stack([np.concatenate(a, axis=1) for a in toks])
    return {"yp": p.reshape(N, 128, L).astype(np.float32), "yq": x.reshape(N, 128, L).astype(np.float32).astype(BF), "yt": yt.astype(np.float32)}

@@ -1,0 +1,400 @@
+import numpy as np
+from concourse.mybir import AluOpType, ActivationFunctionType
+
+A = AluOpType
+F = ActivationFunctionType
+NL = 64
+NS = 16
+NC = 3
+STEPS = 6
+PL = 4096
+BIG = 12582912.0
+P = {
+    "K": (("S", 32), ("S", 32)),
+    "E": (("S", 40), ("V", 24)),
+    "M": (64,),
+    "look": 0.2, "seed": 0, "noise": 0.0,
+    "cy": 0.83e-3 * 1.2, "gather": 1.5, "hop": 0.08, "net": 2.2, "pe": 0.6e-3, "fix": 0.03,
+}
+
+BF, F3, I3, U1, H1 = "bfloat16", "float32", "int32", "uint16", "float16"
+SCRATCH = {
+    "key_s": ("sbuf", [128, 4096], BF), "em_s": ("sbuf", [128, 4096], BF), "cl_s": ("sbuf", [128, 4096], I3),
+    "pl_s": ("sbuf", [128, 192], I3), "emb_s": ("sbuf", [128, 16], BF), "w_s": ("sbuf", [128, 1], BF), "th_s": ("sbuf", [128, 1], F3),
+    "pin": ("sbuf", [128, 7 * 192], U1), "qin": ("sbuf", [128, 7 * 192], BF),
+    "pout": ("sbuf", [128, 6 * 192], U1), "pw": ("sbuf", [128, 6 * 192], U1), "qout": ("sbuf", [128, 6 * 192], BF),
+    "yp_s": ("sbuf", [128, 192], F3), "yt_s": ("sbuf", [128, 1152], F3),
+    "wk": ("sbuf", [128, 2048], BF), "w2": ("sbuf", [128, 2048], BF),
+    "tw": ("sbuf", [128, 8], BF), "bdc": ("sbuf", [128, 8], F3),
+    "bdh": ("sbuf", [128, 128], H1), "idh": ("sbuf", [128, 128], H1), "c1023": ("sbuf", [128, 64], H1),
+    "rep": ("sbuf", [128, 64], U1), "rst32": ("sbuf", [128, 128], F3),
+}
+for _n in ("ones", "bd", "idm", "ltm", "gw0", "gw", "sg", "nbd", "i16", "ihf", "in2k", "bdw", "eb"):
+    SCRATCH[_n] = ("sbuf", [128, 128], BF)
+for _n in ("mb", "mb2", "cb", "ck", "ckb", "cq"):
+    SCRATCH[_n] = ("sbuf", [128, 64], BF)
+for _n in ("icol", "kint", "gint"):
+    SCRATCH[_n] = ("sbuf", [128, 1], I3)
+for _n in ("kcol", "gcol", "sgcol"):
+    SCRATCH[_n] = ("sbuf", [128, 1], F3)
+for _n, _d in (("rowm", F3), ("rowl", I3), ("rowb", F3), ("zero", F3), ("big16", F3)):
+    SCRATCH[_n] = ("sbuf", [128, 64], _d)
+for _c in range(NC):
+    for _n, _w, _d in (("kg", 1024, BF), ("mx", 1024, BF), ("eg", 1024, BF), ("pi", 64, I3), ("pc", 64, I3), ("nr", 64, BF), ("fr", 64, BF),
+                       ("xx", 64, H1), ("hy", 64, F3), ("hn", 64, BF), ("sc", 128, F3), ("ci", 4, U1), ("tt", 64, F3), ("pf", 64, F3),
+                       ("s1", 64, I3), ("s2", 64, I3), ("vt", 64, F3), ("vs", 80, F3), ("oh", 64, BF), ("ot", 64, BF)):
+        SCRATCH["%s%d" % (_n, _c)] = ("sbuf", [128, _w], _d)
+    SCRATCH["psd%d" % _c] = ("psum", [128, 512], F3)
+    SCRATCH["psx%d" % _c] = ("psum", [128, 512], F3)
+
+SEMAPHORES = (["sV", "sS", "sP", "sG", "lsem", "outs"] + ["ld_" + n for n in ("key", "em", "cl", "cl2", "pl", "q", "emb", "w", "th")]
+              + ["a%s%d_%d" % (k, c, t) for k in "pq" for c in range(NC) for t in range(1, STEPS + 1)])
+
+
+def plan(ops):
+    n = len(ops)
+    rng = np.random.RandomState(P["seed"])
+    succ = [[] for _ in range(n)]
+    for o in ops:
+        for d in o["deps"] | o["order"]:
+            succ[d].append(o["n"])
+    prio = [0.0] * n
+    for i in range(n - 1, -1, -1):
+        o = ops[i]
+        prio[i] = o["busy"] + o["lat"] + P["hop"] + max([prio[s] for s in succ[i]] + [0.0])
+    if P["noise"]:
+        prio = [p + P["noise"] * float(r) for p, r in zip(prio, rng.standard_normal(n))]
+    missing = [len(o["deps"] | o["order"]) for o in ops]
+    ready = [0.0] * n
+    free = {}
+    start = [0.0] * n
+    cand = [i for i in range(n) if missing[i] == 0]
+    while cand:
+        best, rows = None, []
+        for i in cand:
+            e = ops[i]["eng"]
+            s = ready[i] if e == "NET" else max(free.get(e, 0.0), ready[i])
+            rows.append((s, i, e))
+            if best is None or s < best[0]:
+                best = (s, i, e)
+        lim = best[0] + min(P["look"], ops[best[1]]["busy"])
+        s, i, e = max((r for r in rows if r[2] == best[2] and r[0] <= lim), key=lambda r: (prio[r[1]], -r[1]))
+        o = ops[i]
+        start[i] = s
+        if e != "NET":
+            free[e] = s + o["busy"]
+        fin = s + o["busy"] + o["lat"]
+        cand.remove(i)
+        for j in succ[i]:
+            missing[j] -= 1
+            ready[j] = max(ready[j], fin + P["hop"] if i in ops[j]["deps"] else s)
+            if missing[j] == 0:
+                cand.append(j)
+    return start, max(start[i] + ops[i]["busy"] + ops[i]["lat"] for i in range(n))
+
+
+def build(g, core, T, topo):
+    rank = T.rank_of(core)
+    cores = T.cores
+    N = len(cores)
+    V, S, PE, Y = g.vector, g.scalar, g.tensor, g.sync
+    CY, FIX = P["cy"], P["fix"]
+    ops = []
+    lastw, readers, banks = {}, {}, {}
+
+    def op(eng, emit, reads=(), writes=(), bank=None, busy=0.1, lat=0.0, sem=None, val=0):
+        i = len(ops)
+        deps, order = set(), set()
+        for k in tuple(reads) + tuple(writes):
+            if k in lastw:
+                deps.add(lastw[k])
+        for k in writes:
+            deps.update(readers.get(k, ()))
+        if bank:
+            h = banks.setdefault(bank, {})
+            for e, j in h.items():
+                (order if e == eng else deps).add(j)
+            h[eng] = i
+        for k in reads:
+            readers.setdefault(k, set()).add(i)
+        for k in writes:
+            lastw[k] = i
+            readers[k] = set()
+        ops.append({"n": i, "eng": eng, "emit": emit, "deps": deps, "order": order - deps, "busy": busy, "lat": lat, "sem": sem, "val": val})
+        return i
+
+    def vd(cyc):
+        return max(64, cyc) * CY + FIX
+
+    def vts(out, in0, s1, s2, op0, op1, reads, writes, cyc=64, bank=None):
+        if op1 is None:
+            op("V", lambda: V.tensor_scalar(out, in0, s1, None, op0), reads, writes, bank, vd(cyc))
+        else:
+            op("V", lambda: V.tensor_scalar(out, in0, s1, s2, op0, op1), reads, writes, bank, vd(cyc))
+
+    def vtt(out, in0, in1, o, reads, writes, cyc=64, bank=None):
+        op("V", lambda: V.tensor_tensor(out, in0, in1, o), reads, writes, bank, vd(cyc))
+
+    def vcp(out, in_, reads, writes, cyc=64, bank=None):
+        op("V", lambda: V.tensor_copy(out, in_), reads, writes, bank, vd(cyc))
+
+    def vfill(ap, x, reads, writes, cyc=64):
+        op("V", lambda: V.memset(ap, x), reads, writes, None, vd(cyc))
+
+    def scan(out, d0, d1, o0, o1, reads, writes, cyc=64, bank=None):
+        op("V", lambda: V.tensor_tensor_scan(out, d0, d1, 0.0, o0, o1), reads, writes, bank, vd(cyc))
+
+    def sact(out, in_, f, reads, writes, bank=None, cyc=64, **kw):
+        op("S", lambda: S.activation(out, in_, f, **kw), reads, writes, bank, cyc * CY + 0.04)
+
+    def gc(fn, writes, reads=(), busy=0.45):
+        op("G", fn, reads, writes, None, busy)
+
+    def mms(lst, reads, bank):
+        def emit():
+            r = None
+            for (o, l, x, a, b) in lst:
+                r = PE.matmul(o, l, x, a, b)
+            return r
+        op("P", emit, reads, (), bank, len(lst) * 64 * P["pe"] + 0.05)
+
+    def load(q, out, in_, name, key, lat):
+        op(q, lambda: (Y if q == "Y" else S).dma_start(out, in_), (), (key,), None, 0.1, lat, "ld_" + name, 16)
+
+    load("Y", T.pl_s[:], T.pl[:], "pl", "pl_s", 2.0)
+    load("S", T.qin[:, 0:192], T.q[:], "q", "q0", 2.2)
+    load("Y", T.key_s[:], T.key[:], "key", "key", 5.0)
+    load("S", T.w_s[:], T.w[:], "w", "w", 2.5)
+    load("S", T.th_s[:], T.th[:], "th", "th", 2.5)
+    load("S", T.emb_s[:], T.emb[:], "emb", "emb", 2.5)
+    load("Y", T.cl_s[:, 0:2048], T.cl[:], "cl", "cl", 8.0)
+    load("Y", T.cl_s[:, 2048:4096], T.cl[:], "cl2", "cl2", 11.0)
+    load("Y", T.em_s[:], T.em[:], "em", "em", 14.0)
+
+    one64 = T.ones[:, 0:64]
+    vfill(T.ones[:], 1.0, (), ("ones",))
+    gc(lambda: g.iota(T.icol[:], [[0, 1]], 0, 1), ("icol",), (), 0.2)
+    gc(lambda: g.affine_select(T.bd[:], T.ones[:], [[-16, 8], [0, 16]], A.is_ge, 0.0, 0, 1), ("bd",), ("ones",))
+    gc(lambda: g.affine_select(T.bd[:], T.bd[:], [[16, 8], [0, 16]], A.is_ge, 0.0, 15, -1), ("bd",))
+    gc(lambda: g.iota(T.rowl[:], [[1, 64]], 0, 0), ("rowl",), (), 0.3)
+    gc(lambda: g.affine_select(T.idm[:], T.ones[:], [[-1, 128]], A.is_equal, 0.0, 0, 1), ("idm",), ("ones",))
+    gc(lambda: g.affine_select(T.ltm[:], T.bd[:], [[1, 128]], A.is_gt, 0.0, 0, -1), ("ltm",), ("bd",))
+    gc(lambda: g.iota(T.rowm[:], [[0, 4], [1, 16]], 0, 0, allow_small_or_imprecise_dtypes=True), ("rowm",), (), 0.3)
+    vfill(T.wk[:], 0.0, (), ("wk0",), 1024)
+    vfill(T.w2[:], 0.0, (), ("w20",), 1024)
+    for c in range(NC):
+        vcp(T.pin[:, 64 * c:64 * c + 64], T.pl_s[:, 64 * c:64 * c + 64], ("pl_s",), ("p%d_0" % c,))
+    vts(T.kint[:], T.icol[:], 15, None, A.bitwise_and, None, ("icol",), ("kint",))
+    vcp(T.kcol[:], T.kint[:], ("kint",), ("kcol",))
+    vcp(T.rep[:], T.rowl[:], ("rowl",), ("rep",))
+    r8 = range(8)
+    wkk, w2k, ebk = tuple("wk%d" % b for b in r8), tuple("w2_%d" % b for b in r8), tuple("eb%d" % b for b in r8)
+    for b in r8:
+        sl = slice(16 * b, 16 * b + 129 * 15 + 1, 129)
+        sact(T.wk[:, sl], T.bd[:, 16 * b:16 * b + 16], F.Copy, ("bd", "wk0"), (wkk[b],), scale=-1.0)
+        vts(T.w2[:, sl], T.bd[:, 16 * b:16 * b + 16], 2.0, None, A.mult, None, ("bd", "w20"), (w2k[b],))
+    vts(T.nbd[:], T.bd[:], -1.0, None, A.mult, None, ("bd",), ("nbd",))
+    vts(T.bdw[:], T.bd[:], T.w_s[:, 0:1], None, A.mult, None, ("bd", "w"), ("bdw",))
+    vcp(T.idh[:], T.idm[:], ("idm",), ("idh",))
+    vts(T.c1023[:], one64, -1023.5, None, A.mult, None, ("ones",), ("c1023",))
+    vfill(T.cb[:], -524288.0, (), ("cb",))
+    vts(T.in2k[:], T.idm[:], -2048.0, None, A.mult, None, ("idm",), ("in2k",))
+    vts(T.mb[:], T.rowm[:], T.kcol[:, 0:1], -4096.0, A.is_equal, A.mult, ("rowm", "kcol"), ("mb",))
+    vts(T.mb2[:], T.mb[:], -2048.0, None, A.add, None, ("mb",), ("mb2",))
+    vtt(T.gw0[:], T.idm[:], T.ltm[:], A.subtract, ("idm", "ltm"), ("gw0",), 256)
+    vts(T.gw[:], T.gw0[:], 4096.0, None, A.mult, None, ("gw0",), ("gw",))
+    vts(T.sgcol[:], T.kcol[:], -4096.0, 57344.0, A.mult, A.add, ("kcol",), ("sgcol",))
+    vts(T.sg[:], T.bd[:], T.sgcol[:, 0:1], None, A.mult, None, ("bd", "sgcol"), ("sg",))
+    vcp(T.bdh[:], T.bd[:], ("bd",), ("bdh",))
+    vfill(T.rst32[:], 1.0, (), ("rst32",), 128)
+    vfill(T.rst32[:, 0:128:32], 0.0, (), ("rst32",))
+    vts(T.i16[:], T.idm[:], 16.0, None, A.mult, None, ("idm",), ("i16",))
+    vts(T.ck[:], one64, T.kcol[:, 0:1], -1.0, A.mult, A.mult, ("ones", "kcol"), ("ck",))
+    vts(T.gint[:], T.icol[:], 4, 1, A.logical_shift_right, A.bitwise_and, ("icol",), ("gint",))
+    vts(T.gcol[:], T.gint[:], 65536.0, None, A.mult, None, ("gint",), ("gcol",))
+    vfill(T.rowb[:, 0:32], 0.0, (), ("rowb0",))
+    vfill(T.rowb[:, 32:64], 131072.0, (), ("rowb1",))
+    vts(T.ckb[:], T.rowb[:], T.gcol[:, 0:1], None, A.add, None, ("rowb0", "rowb1", "gcol"), ("ckb",))
+    vfill(T.zero[:], 0.0, (), ("zero",))
+    vfill(T.big16[:], 0.0, (), ("big16",))
+    vfill(T.big16[:, 0:64:16], 8388608.0, (), ("big16",))
+    for c in range(NC):
+        vfill(T["vs%d" % c][:, 64:80], 4194304.0, (), ("vsp%d" % c,))
+    vts(T.ihf[:], T.idm[:], 0.5, None, A.mult, None, ("idm",), ("ihf",))
+    vfill(T.cq[:], -0.25, (), ("cq",))
+    vcp(T.bdc[:], T.bd[:, 0:128:16], ("bd",), ("bdc",))
+    vts(T.tw[:], T.bdc[:], T.kcol[:, 0:1], None, A.mult, None, ("bdc", "kcol"), ("tw",))
+    for b in r8:
+        vts(T.eb[:, 16 * b:16 * b + 16], T.emb_s[:], T.bdc[:, b:b + 1], 0.5, A.mult, A.mult, ("emb", "bdc"), (ebk[b],))
+
+    def gather(e, out, win, off, reads, writes, count):
+        fn = (lambda: S.activation(out, win.indirect(off), F.Copy)) if e == "S" else (lambda: V.tensor_copy(out, win.indirect(off)))
+        op(e, fn, reads, writes, None, 0.07 + count * P["gather"] * CY)
+
+    sends = [0]
+
+    def send(dst, out, in_, sem, key, akey):
+        eng = topo.engines(core, dst)[:8]
+        rid, pid, _ = topo.addr(dst)
+        m = sum(1 << x for x in eng)
+        sends[0] += len(eng)
+        i = op("G", lambda: g.remote_dma(out, in_, T.sem[sem], T.sem.lsem, pid, rid, m), (key,), (), None, 0.15)
+        ops[i]["remote"] = True
+        j = op("NET", None, (), (akey,), None, 0.0, P["net"], sem, len(eng))
+        ops[j]["deps"].add(i)
+
+    def step(t, c):
+        B = lambda n: T["%s%d" % (n, c)]
+        k = lambda n: "%s%d" % (n, c)
+        o0 = t * 192 + NL * c
+        o1 = o0 + 192
+        pin, qin = T.pin[:, o0:o0 + NL], T.qin[:, o0:o0 + NL]
+        pkey = "p%d_%d" % (c, t)
+        qkey = "q%d_%d" % (c, t) if t else "q0"
+        psd, psx = B("psd"), B("psx")
+        bd, bx = "D%d" % c, "X%d" % c
+        kg, mx, eg = B("kg"), B("mx"), B("eg")
+        D, U, AR = psd[:, 0:64], psd[:, 64:128], psd[:, 128:192]
+        CH, C0, C1 = psx[:, 0:128], psx[:, 0:128:2], psx[:, 1:128:2]
+        HA, VO, QO, TK, V2 = psx[:, 128:192], psx[:, 192:256], psx[:, 256:320], psx[0:8, 320:384], psx[:, 384:448]
+        kgk, a = [], 0
+        for e, w in P["K"]:
+            kgk.append("%s_%d" % (k("kg"), a))
+            gather(e, kg[:, 16 * a:16 * (a + w)], T.key_s[:], T.pin[:, o0 + a:o0 + a + w], ("key", pkey), (kgk[-1],), 16 * w)
+            a += w
+        kgk = tuple(kgk)
+        if t == 0:
+            pi, pik = T.pl_s[:, NL * c:NL * c + NL], "pl_s"
+        else:
+            pi, pik = B("pi")[:], k("pi")
+            vcp(pi, pin, (pkey,), (pik,))
+        vts(B("pc")[:], pi, 1, None, A.logical_shift_right, None, (pik,), (k("pc"),))
+        mms([(D, T.wk[:, 128 * i:128 * i + 128], kg[:, i:1024:16], i == 0, False) for i in range(NS)], kgk + wkk, bd)
+        mms([(D, T.nbd[:], qin, False, False)], ("nbd", qkey), bd)
+        mxk, a = [], 0
+        for w in P["M"]:
+            mxk.append("%s_%d" % (k("mx"), a))
+            op("V", lambda s=slice(16 * a, 16 * (a + w)), a=a, w=w: V.tensor_tensor(mx[:, s], qin.indirect(T.rep[:, a:a + w]), kg[:, s], A.max),
+               ("rep", qkey) + kgk, (mxk[-1],), None, 0.06 + 16 * w * P["gather"] * CY)
+            a += w
+        mms([(HA, T.bdw[:], qin, True, False), (HA, T.idh[:], T.c1023[:], False, False), (HA, T.idm[:], T.cb[:], False, True)],
+            ("bdw", "idh", "c1023", "idm", "cb", qkey), bx)
+        sact(B("hy")[:], HA, F.Identity, (), (k("hy"),), bx, bias=BIG, scale=1.0 / 2048.0)
+        sact(B("hn")[:], B("hy")[:], F.Identity, (k("hy"),), (k("hn"),), bias=-BIG)
+        mms([(C1, T.bdw[:], qin, True, False), (C1, T.idm[:], T.mb2[:], False, False), (C1, T.idm[:], T.cb[:], False, False),
+             (C1, T.in2k[:], B("hn")[:], False, True)], ("in2k", "mb2", k("hn")), bx)
+        mms([(D, T.w2[:, 128 * i:128 * i + 128], mx[:, i:1024:16], False, i == NS - 1) for i in range(NS)], tuple(mxk) + w2k, bd)
+        vts(B("nr")[:], D, T.th_s[:, 0:1], None, A.is_lt, None, ("th",), (k("nr"),), 64, bd)
+        mms([(U, T.gw[:], B("nr")[:], True, True)], ("gw", k("nr")), bd)
+        mms([(C0, T.idm[:], T.mb[:], True, False), (C0, T.sg[:], B("nr")[:], False, False)], ("idm", "mb", "sg", k("nr")), bx)
+        sact(B("fr")[:], B("nr")[:], F.Identity, (k("nr"),), (k("fr"),), bias=1.0, scale=-1.0)
+        vtt(B("xx")[:], U, B("pc")[:], A.min, (k("pc"),), (k("xx"),), 64, bd)
+        mms([(C0, T.bdh[:], B("xx")[:], False, True)], ("bdh", k("xx")), bx)
+        vtt(AR, B("nr")[:], pi, A.mult, (k("nr"), pik), (k("ar"),), 128, bd)
+        scan(B("sc")[:], T.rst32[:], CH, A.mult, A.min, ("rst32",), (k("sc"),), 128, bx)
+        vts(B("ci")[:], B("sc")[:, 31:128:32], 8192.0, None, A.add, None, (k("sc"),), (k("ci"),))
+        op("V", lambda: V.tensor_tensor(B("tt")[:], T.cl_s[:].indirect(B("ci")[:, 0:4]), B("fr")[:], A.mult),
+           ("cl", "cl2", k("ci"), k("fr")), (k("tt"),), None, 0.06 + 64 * P["gather"] * CY)
+        vtt(B("pf")[:], AR, B("tt")[:], A.add, (k("tt"), k("ar")), (k("pf"),), 64, bd)
+        pok = "po%d_%d" % (c, t)
+        vcp(T.pout[:, o0:o0 + NL], B("pf")[:], (k("pf"),), (pok,))
+        nxt = cores[(rank + 1) % N if c == 0 else (rank - 1) % N]
+        shift = 1 if (c == 0 and rank == N - 1) else (PL - 1 if (c and rank == 0) else 0)
+        src, sk = T.pout[:, o0:o0 + NL], pok
+        if shift:
+            src, sk = T.pw[:, o0:o0 + NL], "pw%d_%d" % (c, t)
+            vts(B("s1")[:], B("pf")[:], float(shift), None, A.add, None, (k("pf"),), (k("s1"),))
+            vts(B("s2")[:], B("s1")[:], PL - 1, None, A.bitwise_and, None, (k("s1"),), (k("s2"),))
+            vcp(src, B("s2")[:], (k("s2"),), (sk,))
+        send(nxt, T.pin[:, o1:o1 + NL], src, "ap%d_%d" % (c, t + 1), sk, "p%d_%d" % (c, t + 1))
+        egk, a = [], 0
+        for e, w in P["E"]:
+            egk.append("%s_%d" % (k("eg"), a))
+            gather(e, eg[:, 16 * a:16 * (a + w)], T.em_s[:], T.pout[:, o0 + a:o0 + a + w], ("em", pok), (egk[-1],), 16 * w)
+            a += w
+        mms([(VO, T.idm[:], T.ck[:], True, False), (VO, T.idm[:], T.ckb[:], False, False)], ("idm", "ck", "ckb"), bx)
+        mms([(VO, T.i16[:], eg[:, i:1024:16], False, i == NS - 1) for i in range(NS)], tuple(egk) + ("i16",), bx)
+        op("V", lambda: V.transpose(B("vt")[:], VO), (), (k("vt"),), bx, vd(64))
+        mms([(QO, T.idm[:], T.cq[:], True, False), (QO, T.ihf[:], qin, False, False)], ("idm", "cq", "ihf", qkey), bx)
+        scan(B("vs")[:, 0:64], T.zero[:], B("vt")[:], A.max, A.max, ("zero", k("vt")), (k("vs"),))
+        scan(V2, T.big16[:], B("vs")[:, 15:79], A.max, A.min, ("big16", k("vs"), k("vsp")), (k("v2"),), 64, bx)
+        vtt(B("oh")[:], B("vt")[:], V2, A.is_equal, (k("vt"), k("v2")), (k("oh"),), 64, bx)
+        op("V", lambda: V.transpose(B("ot")[:], B("oh")[:]), (k("oh"),), (k("ot"),), None, vd(64))
+        mms([(QO, T.eb[:], B("ot")[:], False, True)], ebk + (k("ot"),), bx)
+        mms([(TK, T.tw[:], B("ot")[:], True, True)], ("tw", k("ot")), bx)
+        qok = "qo%d_%d" % (c, t)
+        vts(T.qout[:, o0:o0 + NL], QO, BIG, BIG, A.add, A.subtract, (), (qok,), 64, bx)
+        sact(T.yt_s[0:8, o0:o0 + NL], TK, F.Copy, (), ("yt%d_%d" % (c, t),), bx)
+        send(nxt, T.qin[:, o1:o1 + NL], T.qout[:, o0:o0 + NL], "aq%d_%d" % (c, t + 1), qok, "q%d_%d" % (c, t + 1))
+
+    for t in range(STEPS):
+        for c in range(NC):
+            step(t, c)
+    nout = [0]
+
+    def store(out, in_, reads):
+        nout[0] += 16
+        op("Y", lambda: Y.dma_start(out, in_), reads, (), None, 0.1, 2.0, "outs", None)
+
+    o6 = STEPS * 192
+    for c in range(NC):
+        a, b = NL * c, NL * c + NL
+        vcp(T.yp_s[:, a:b], T.pin[:, o6 + a:o6 + b], ("p%d_%d" % (c, STEPS),), ("yp%d" % c,))
+        store(T.yp[:, a:b], T.yp_s[:, a:b], ("yp%d" % c,))
+        store(T.yq[:, a:b], T.qin[:, o6 + a:o6 + b], ("q%d_%d" % (c, STEPS),))
+    store(T.yt[:], T.yt_s[0:8, :], tuple("yt%d_%d" % (c, t) for c in range(NC) for t in range(STEPS)))
+    return ops, sends[0], nout[0]
+
+
+def emit_all(g, T, ops, start, nsend, nout):
+    eng = {"V": g.vector, "S": g.scalar, "P": g.tensor, "G": g, "Y": g.sync}
+    esem = {"V": "sV", "S": "sS", "P": "sP", "G": "sG"}
+    count = {e: 0 for e in eng}
+    known = {e: {} for e in eng}
+    fin = {}
+    for i in sorted(range(len(ops)), key=lambda x: (start[x], x)):
+        o = ops[i]
+        e = o["eng"]
+        if e == "NET":
+            fin[i] = (o["sem"], o["val"], {o["sem"]: o["val"]})
+            continue
+        kn = known[e]
+        need = {}
+        for d in o["deps"]:
+            s, v, _ = fin[d]
+            if kn.get(s, 0) < v and need.get(s, (0, None))[0] < v:
+                need[s] = (v, d)
+        for s in list(need):
+            v = need[s][0]
+            if any(s2 != s and fin[need[s2][1]][2].get(s, 0) >= v for s2 in need):
+                del need[s]
+        for s in sorted(need):
+            v, d = need[s]
+            eng[e].wait_ge(T.sem[s], v)
+            for s2, v2 in fin[d][2].items():
+                if kn.get(s2, 0) < v2:
+                    kn[s2] = v2
+        ins = o["emit"]()
+        c = dict(kn)
+        if o["sem"] is not None:
+            ins.then_inc(T.sem[o["sem"]], 16)
+            if o["val"]:
+                c[o["sem"]] = o["val"]
+            fin[i] = (o["sem"], o["val"], c)
+        elif not o.get("remote"):
+            count[e] += 1
+            ins.then_inc(T.sem[esem[e]], 1)
+            c[esem[e]] = count[e]
+            fin[i] = (esem[e], count[e], c)
+    g.wait_ge(T.sem.lsem, nsend)
+    for e in ("V", "S", "P", "G"):
+        g.wait_ge(T.sem[esem[e]], count[e])
+    g.sync.wait_ge(T.sem.outs, nout)
+
+
+def rank_program(g, core, T, topo):
+    if T.rank_of(core) is None:
+        return
+    ops, nsend, nout = build(g, core, T, topo)
+    start, _ = plan(ops)
+    emit_all(g, T, ops, start, nsend, nout)

@@ -10,16 +10,16 @@ STEPS = 6
 PL = 4096
 BIG = 12582912.0
 P = {
-    "K": (("S", 32), ("S", 32)),
-    "E": (("S", 40), ("V", 24)),
+    "K": (("S", 64),),
+    "E": (("S", 48), ("V", 16)),
     "M": (64,),
-    "look": 0.2, "seed": 0, "noise": 0.0,
-    "cy": 0.83e-3 * 1.2, "gather": 1.5, "hop": 0.08, "net": 2.2, "pe": 0.6e-3, "fix": 0.03,
+    "look": 0.1, "seed": 0, "noise": 0.0, "stag": (0.0, 0.0, 0.0),
+    "cy": 0.83e-3 * 1.2, "gather": 1.5, "hop": 0.1, "net": 2.6, "pe": 0.55e-3, "fix": 0.02,
 }
 
 BF, F3, I3, U1, H1 = "bfloat16", "float32", "int32", "uint16", "float16"
 SCRATCH = {
-    "key_s": ("sbuf", [128, 4096], BF), "em_s": ("sbuf", [128, 4096], BF), "cl_s": ("sbuf", [128, 4096], I3),
+    "key_s": ("sbuf", [128, 4096], BF), "em_s": ("sbuf", [128, 4096], BF), "cl_s": ("sbuf", [128, 2048], I3),
     "pl_s": ("sbuf", [128, 192], I3), "emb_s": ("sbuf", [128, 16], BF), "w_s": ("sbuf", [128, 1], BF), "th_s": ("sbuf", [128, 1], F3),
     "pin": ("sbuf", [128, 7 * 192], U1), "qin": ("sbuf", [128, 7 * 192], BF),
     "pout": ("sbuf", [128, 6 * 192], U1), "pw": ("sbuf", [128, 6 * 192], U1), "qout": ("sbuf", [128, 6 * 192], BF),
@@ -29,7 +29,7 @@ SCRATCH = {
     "bdh": ("sbuf", [128, 128], H1), "idh": ("sbuf", [128, 128], H1), "c1023": ("sbuf", [128, 64], H1),
     "rep": ("sbuf", [128, 64], U1), "rst32": ("sbuf", [128, 128], F3),
 }
-for _n in ("ones", "bd", "idm", "ltm", "gw0", "gw", "sg", "nbd", "i16", "ihf", "in2k", "bdw", "eb"):
+for _n in ("ones", "bd", "idm", "ltm", "gw0", "gw", "sg", "nbd", "bd4k", "i16", "i8k", "ihf", "in2k", "bdw", "eb"):
     SCRATCH[_n] = ("sbuf", [128, 128], BF)
 for _n in ("mb", "mb2", "cb", "ck", "ckb", "cq"):
     SCRATCH[_n] = ("sbuf", [128, 64], BF)
@@ -40,14 +40,14 @@ for _n in ("kcol", "gcol", "sgcol"):
 for _n, _d in (("rowm", F3), ("rowl", I3), ("rowb", F3), ("zero", F3), ("big16", F3)):
     SCRATCH[_n] = ("sbuf", [128, 64], _d)
 for _c in range(NC):
-    for _n, _w, _d in (("kg", 1024, BF), ("mx", 1024, BF), ("eg", 1024, BF), ("pi", 64, I3), ("pc", 64, I3), ("nr", 64, BF), ("fr", 64, BF),
-                       ("xx", 64, H1), ("hy", 64, F3), ("hn", 64, BF), ("sc", 128, F3), ("ci", 4, U1), ("tt", 64, F3), ("pf", 64, F3),
-                       ("s1", 64, I3), ("s2", 64, I3), ("vt", 64, F3), ("vs", 80, F3), ("oh", 64, BF), ("ot", 64, BF)):
+    for _n, _w, _d in (("kg", 1024, BF), ("mx", 1024, BF), ("eg", 1024, BF), ("ph", 64, H1), ("pc", 64, I3), ("nr", 64, BF), ("ar", 64, F3),
+                       ("xx", 64, H1), ("hy", 64, F3), ("hn", 64, BF), ("sc", 128, F3), ("ci", 4, U1), ("pf", 64, I3),
+                       ("s1", 64, I3), ("s2", 64, I3), ("s3", 64, I3), ("vt", 64, F3), ("vs", 80, F3), ("oh", 64, BF), ("ot", 64, BF)):
         SCRATCH["%s%d" % (_n, _c)] = ("sbuf", [128, _w], _d)
     SCRATCH["psd%d" % _c] = ("psum", [128, 512], F3)
     SCRATCH["psx%d" % _c] = ("psum", [128, 512], F3)
 
-SEMAPHORES = (["sV", "sS", "sP", "sG", "lsem", "outs"] + ["ld_" + n for n in ("key", "em", "cl", "cl2", "pl", "q", "emb", "w", "th")]
+SEMAPHORES = (["sV", "sS", "sP", "sG", "lsem", "outs"] + ["ld_" + n for n in ("key", "em", "cl", "pl", "q", "emb", "w", "th")]
               + ["a%s%d_%d" % (k, c, t) for k in "pq" for c in range(NC) for t in range(1, STEPS + 1)])
 
 
@@ -62,6 +62,7 @@ def plan(ops):
     for i in range(n - 1, -1, -1):
         o = ops[i]
         prio[i] = o["busy"] + o["lat"] + P["hop"] + max([prio[s] for s in succ[i]] + [0.0])
+    prio = [p - P["stag"][o["c"]] for p, o in zip(prio, ops)]
     if P["noise"]:
         prio = [p + P["noise"] * float(r) for p, r in zip(prio, rng.standard_normal(n))]
     missing = [len(o["deps"] | o["order"]) for o in ops]
@@ -101,6 +102,7 @@ def build(g, core, T, topo):
     CY, FIX = P["cy"], P["fix"]
     ops = []
     lastw, readers, banks = {}, {}, {}
+    cur = [0]
 
     def op(eng, emit, reads=(), writes=(), bank=None, busy=0.1, lat=0.0, sem=None, val=0):
         i = len(ops)
@@ -120,7 +122,7 @@ def build(g, core, T, topo):
         for k in writes:
             lastw[k] = i
             readers[k] = set()
-        ops.append({"n": i, "eng": eng, "emit": emit, "deps": deps, "order": order - deps, "busy": busy, "lat": lat, "sem": sem, "val": val})
+        ops.append({"n": i, "eng": eng, "emit": emit, "deps": deps, "order": order - deps, "busy": busy, "lat": lat, "sem": sem, "val": val, "c": cur[0]})
         return i
 
     def vd(cyc):
@@ -167,9 +169,8 @@ def build(g, core, T, topo):
     load("S", T.w_s[:], T.w[:], "w", "w", 2.5)
     load("S", T.th_s[:], T.th[:], "th", "th", 2.5)
     load("S", T.emb_s[:], T.emb[:], "emb", "emb", 2.5)
-    load("Y", T.cl_s[:, 0:2048], T.cl[:], "cl", "cl", 8.0)
-    load("Y", T.cl_s[:, 2048:4096], T.cl[:], "cl2", "cl2", 11.0)
-    load("Y", T.em_s[:], T.em[:], "em", "em", 14.0)
+    load("Y", T.cl_s[:], T.cl[:], "cl", "cl", 8.0)
+    load("Y", T.em_s[:], T.em[:], "em", "em", 10.5)
 
     one64 = T.ones[:, 0:64]
     vfill(T.ones[:], 1.0, (), ("ones",))
@@ -193,22 +194,24 @@ def build(g, core, T, topo):
         sl = slice(16 * b, 16 * b + 129 * 15 + 1, 129)
         sact(T.wk[:, sl], T.bd[:, 16 * b:16 * b + 16], F.Copy, ("bd", "wk0"), (wkk[b],), scale=-1.0)
         vts(T.w2[:, sl], T.bd[:, 16 * b:16 * b + 16], 2.0, None, A.mult, None, ("bd", "w20"), (w2k[b],))
-    vts(T.nbd[:], T.bd[:], -1.0, None, A.mult, None, ("bd",), ("nbd",))
+    sact(T.nbd[:], T.bd[:], F.Copy, ("bd",), ("nbd",), None, 128, scale=-1.0)
     vts(T.bdw[:], T.bd[:], T.w_s[:, 0:1], None, A.mult, None, ("bd", "w"), ("bdw",))
     vcp(T.idh[:], T.idm[:], ("idm",), ("idh",))
     vts(T.c1023[:], one64, -1023.5, None, A.mult, None, ("ones",), ("c1023",))
     vfill(T.cb[:], -524288.0, (), ("cb",))
-    vts(T.in2k[:], T.idm[:], -2048.0, None, A.mult, None, ("idm",), ("in2k",))
-    vts(T.mb[:], T.rowm[:], T.kcol[:, 0:1], -4096.0, A.is_equal, A.mult, ("rowm", "kcol"), ("mb",))
-    vts(T.mb2[:], T.mb[:], -2048.0, None, A.add, None, ("mb",), ("mb2",))
+    sact(T.in2k[:], T.idm[:], F.Copy, ("idm",), ("in2k",), None, 128, scale=-2048.0)
+    sact(T.i8k[:], T.idm[:], F.Copy, ("idm",), ("i8k",), None, 128, scale=8192.0)
+    sact(T.bd4k[:], T.bd[:], F.Copy, ("bd",), ("bd4k",), None, 128, scale=4096.0)
+    vts(T.mb2[:], T.rowm[:], T.kcol[:, 0:1], -8192.0, A.is_equal, A.mult, ("rowm", "kcol"), ("mb2",))
+    vts(T.mb[:], T.mb2[:], 4096.0, None, A.add, None, ("mb2",), ("mb",))
     vtt(T.gw0[:], T.idm[:], T.ltm[:], A.subtract, ("idm", "ltm"), ("gw0",), 256)
-    vts(T.gw[:], T.gw0[:], 4096.0, None, A.mult, None, ("gw0",), ("gw",))
+    sact(T.gw[:], T.gw0[:], F.Copy, ("gw0",), ("gw",), None, 128, scale=4096.0)
     vts(T.sgcol[:], T.kcol[:], -4096.0, 57344.0, A.mult, A.add, ("kcol",), ("sgcol",))
     vts(T.sg[:], T.bd[:], T.sgcol[:, 0:1], None, A.mult, None, ("bd", "sgcol"), ("sg",))
     vcp(T.bdh[:], T.bd[:], ("bd",), ("bdh",))
     vfill(T.rst32[:], 1.0, (), ("rst32",), 128)
     vfill(T.rst32[:, 0:128:32], 0.0, (), ("rst32",))
-    vts(T.i16[:], T.idm[:], 16.0, None, A.mult, None, ("idm",), ("i16",))
+    sact(T.i16[:], T.idm[:], F.Copy, ("idm",), ("i16",), None, 128, scale=16.0)
     vts(T.ck[:], one64, T.kcol[:, 0:1], -1.0, A.mult, A.mult, ("ones", "kcol"), ("ck",))
     vts(T.gint[:], T.icol[:], 4, 1, A.logical_shift_right, A.bitwise_and, ("icol",), ("gint",))
     vts(T.gcol[:], T.gint[:], 65536.0, None, A.mult, None, ("gint",), ("gcol",))
@@ -220,7 +223,7 @@ def build(g, core, T, topo):
     vfill(T.big16[:, 0:64:16], 8388608.0, (), ("big16",))
     for c in range(NC):
         vfill(T["vs%d" % c][:, 64:80], 4194304.0, (), ("vsp%d" % c,))
-    vts(T.ihf[:], T.idm[:], 0.5, None, A.mult, None, ("idm",), ("ihf",))
+    sact(T.ihf[:], T.idm[:], F.Copy, ("idm",), ("ihf",), None, 128, scale=0.5)
     vfill(T.cq[:], -0.25, (), ("cq",))
     vcp(T.bdc[:], T.bd[:, 0:128:16], ("bd",), ("bdc",))
     vts(T.tw[:], T.bdc[:], T.kcol[:, 0:1], None, A.mult, None, ("bdc", "kcol"), ("tw",))
@@ -244,6 +247,7 @@ def build(g, core, T, topo):
         ops[j]["deps"].add(i)
 
     def step(t, c):
+        cur[0] = c
         B = lambda n: T["%s%d" % (n, c)]
         k = lambda n: "%s%d" % (n, c)
         o0 = t * 192 + NL * c
@@ -263,12 +267,8 @@ def build(g, core, T, topo):
             gather(e, kg[:, 16 * a:16 * (a + w)], T.key_s[:], T.pin[:, o0 + a:o0 + a + w], ("key", pkey), (kgk[-1],), 16 * w)
             a += w
         kgk = tuple(kgk)
-        if t == 0:
-            pi, pik = T.pl_s[:, NL * c:NL * c + NL], "pl_s"
-        else:
-            pi, pik = B("pi")[:], k("pi")
-            vcp(pi, pin, (pkey,), (pik,))
-        vts(B("pc")[:], pi, 1, None, A.logical_shift_right, None, (pik,), (k("pc"),))
+        vts(B("pc")[:], pin, 0.5, -0.25, A.mult, A.add, (pkey,), (k("pc"),))
+        vts(B("ph")[:], pin, -2048.0, None, A.add, None, (pkey,), (k("ph"),))
         mms([(D, T.wk[:, 128 * i:128 * i + 128], kg[:, i:1024:16], i == 0, False) for i in range(NS)], kgk + wkk, bd)
         mms([(D, T.nbd[:], qin, False, False)], ("nbd", qkey), bd)
         mxk, a = [], 0
@@ -282,30 +282,31 @@ def build(g, core, T, topo):
         sact(B("hy")[:], HA, F.Identity, (), (k("hy"),), bx, bias=BIG, scale=1.0 / 2048.0)
         sact(B("hn")[:], B("hy")[:], F.Identity, (k("hy"),), (k("hn"),), bias=-BIG)
         mms([(C1, T.bdw[:], qin, True, False), (C1, T.idm[:], T.mb2[:], False, False), (C1, T.idm[:], T.cb[:], False, False),
-             (C1, T.in2k[:], B("hn")[:], False, True)], ("in2k", "mb2", k("hn")), bx)
+             (C1, T.in2k[:], B("hn")[:], False, False)], ("in2k", "mb2", k("hn")), bx)
         mms([(D, T.w2[:, 128 * i:128 * i + 128], mx[:, i:1024:16], False, i == NS - 1) for i in range(NS)], tuple(mxk) + w2k, bd)
         vts(B("nr")[:], D, T.th_s[:, 0:1], None, A.is_lt, None, ("th",), (k("nr"),), 64, bd)
         mms([(U, T.gw[:], B("nr")[:], True, True)], ("gw", k("nr")), bd)
-        mms([(C0, T.idm[:], T.mb[:], True, False), (C0, T.sg[:], B("nr")[:], False, False)], ("idm", "mb", "sg", k("nr")), bx)
-        sact(B("fr")[:], B("nr")[:], F.Identity, (k("nr"),), (k("fr"),), bias=1.0, scale=-1.0)
+        mms([(C1, T.bd4k[:], B("nr")[:], False, True), (C0, T.idm[:], T.mb[:], True, False), (C0, T.sg[:], B("nr")[:], False, False)],
+            ("bd4k", "idm", "mb", "sg", k("nr")), bx)
+        mms([(AR, T.idh[:], B("ph")[:], True, False), (AR, T.i8k[:], B("nr")[:], False, True)], ("idh", "i8k", k("nr"), k("ph")), bd)
         vtt(B("xx")[:], U, B("pc")[:], A.min, (k("pc"),), (k("xx"),), 64, bd)
+        sact(B("ar")[:], AR, F.Identity, (), (k("ar"),), bd, bias=-2048.0)
         mms([(C0, T.bdh[:], B("xx")[:], False, True)], ("bdh", k("xx")), bx)
-        vtt(AR, B("nr")[:], pi, A.mult, (k("nr"), pik), (k("ar"),), 128, bd)
         scan(B("sc")[:], T.rst32[:], CH, A.mult, A.min, ("rst32",), (k("sc"),), 128, bx)
         vts(B("ci")[:], B("sc")[:, 31:128:32], 8192.0, None, A.add, None, (k("sc"),), (k("ci"),))
-        op("V", lambda: V.tensor_tensor(B("tt")[:], T.cl_s[:].indirect(B("ci")[:, 0:4]), B("fr")[:], A.mult),
-           ("cl", "cl2", k("ci"), k("fr")), (k("tt"),), None, 0.06 + 64 * P["gather"] * CY)
-        vtt(B("pf")[:], AR, B("tt")[:], A.add, (k("tt"), k("ar")), (k("pf"),), 64, bd)
+        op("V", lambda: V.tensor_tensor(B("pf")[:], T.cl_s[:].indirect(B("ci")[:, 0:4]), B("ar")[:], A.max),
+           ("cl", k("ci"), k("ar")), (k("pf"),), None, 0.06 + 64 * P["gather"] * CY)
+        vts(B("s2")[:], B("pf")[:], PL - 1, None, A.bitwise_and, None, (k("pf"),), (k("s2"),))
         pok = "po%d_%d" % (c, t)
-        vcp(T.pout[:, o0:o0 + NL], B("pf")[:], (k("pf"),), (pok,))
+        vcp(T.pout[:, o0:o0 + NL], B("s2")[:], (k("s2"),), (pok,))
         nxt = cores[(rank + 1) % N if c == 0 else (rank - 1) % N]
         shift = 1 if (c == 0 and rank == N - 1) else (PL - 1 if (c and rank == 0) else 0)
         src, sk = T.pout[:, o0:o0 + NL], pok
         if shift:
             src, sk = T.pw[:, o0:o0 + NL], "pw%d_%d" % (c, t)
             vts(B("s1")[:], B("pf")[:], float(shift), None, A.add, None, (k("pf"),), (k("s1"),))
-            vts(B("s2")[:], B("s1")[:], PL - 1, None, A.bitwise_and, None, (k("s1"),), (k("s2"),))
-            vcp(src, B("s2")[:], (k("s2"),), (sk,))
+            vts(B("s3")[:], B("s1")[:], PL - 1, None, A.bitwise_and, None, (k("s1"),), (k("s3"),))
+            vcp(src, B("s3")[:], (k("s3"),), (sk,))
         send(nxt, T.pin[:, o1:o1 + NL], src, "ap%d_%d" % (c, t + 1), sk, "p%d_%d" % (c, t + 1))
         egk, a = [], 0
         for e, w in P["E"]:

import numpy as np
from concourse.mybir import AluOpType, ActivationFunctionType

A = AluOpType
F = ActivationFunctionType
NL = 64
NS = 16
NC = 3
STEPS = 6
PL = 4096
BIG = 12582912.0
P = {
    "K": (("S", 64),),
    "E": (("S", 48), ("V", 16)),
    "M": (64,),
    "look": 0.1, "seed": 0, "noise": 0.0, "stag": (0.0, 0.0, 0.0),
    "cy": 0.83e-3 * 1.2, "gather": 1.5, "hop": 0.1, "net": 2.6, "pe": 0.55e-3, "fix": 0.02,
}

BF, F3, I3, U1, H1 = "bfloat16", "float32", "int32", "uint16", "float16"
SCRATCH = {
    "key_s": ("sbuf", [128, 4096], BF), "em_s": ("sbuf", [128, 4096], BF), "cl_s": ("sbuf", [128, 2048], I3),
    "pl_s": ("sbuf", [128, 192], I3), "emb_s": ("sbuf", [128, 16], BF), "w_s": ("sbuf", [128, 1], BF), "th_s": ("sbuf", [128, 1], F3),
    "pin": ("sbuf", [128, 7 * 192], U1), "qin": ("sbuf", [128, 7 * 192], BF),
    "pout": ("sbuf", [128, 6 * 192], U1), "pw": ("sbuf", [128, 6 * 192], U1), "qout": ("sbuf", [128, 6 * 192], BF),
    "yp_s": ("sbuf", [128, 192], F3), "yt_s": ("sbuf", [128, 1152], F3),
    "wk": ("sbuf", [128, 2048], BF), "w2": ("sbuf", [128, 2048], BF),
    "tw": ("sbuf", [128, 8], BF), "bdc": ("sbuf", [128, 8], F3),
    "bdh": ("sbuf", [128, 128], H1), "idh": ("sbuf", [128, 128], H1), "c1023": ("sbuf", [128, 64], H1),
    "rep": ("sbuf", [128, 64], U1), "rst32": ("sbuf", [128, 128], F3),
}
for _n in ("ones", "bd", "idm", "ltm", "gw0", "gw", "sg", "nbd", "bd4k", "i16", "i8k", "ihf", "in2k", "bdw", "eb"):
    SCRATCH[_n] = ("sbuf", [128, 128], BF)
for _n in ("mb", "mb2", "cb", "ck", "ckb", "cq"):
    SCRATCH[_n] = ("sbuf", [128, 64], BF)
for _n in ("icol", "kint", "gint"):
    SCRATCH[_n] = ("sbuf", [128, 1], I3)
for _n in ("kcol", "gcol", "sgcol"):
    SCRATCH[_n] = ("sbuf", [128, 1], F3)
for _n, _d in (("rowm", F3), ("rowl", I3), ("rowb", F3), ("zero", F3), ("big16", F3)):
    SCRATCH[_n] = ("sbuf", [128, 64], _d)
for _c in range(NC):
    for _n, _w, _d in (("kg", 1024, BF), ("mx", 1024, BF), ("eg", 1024, BF), ("ph", 64, H1), ("pc", 64, I3), ("nr", 64, BF), ("ar", 64, F3),
                       ("xx", 64, H1), ("hy", 64, F3), ("hn", 64, BF), ("sc", 128, F3), ("ci", 4, U1), ("pf", 64, I3),
                       ("s1", 64, I3), ("s2", 64, I3), ("s3", 64, I3), ("vt", 64, F3), ("vs", 80, F3), ("oh", 64, BF), ("ot", 64, BF)):
        SCRATCH["%s%d" % (_n, _c)] = ("sbuf", [128, _w], _d)
    SCRATCH["psd%d" % _c] = ("psum", [128, 512], F3)
    SCRATCH["psx%d" % _c] = ("psum", [128, 512], F3)

SEMAPHORES = (["sV", "sS", "sP", "sG", "lsem", "outs"] + ["ld_" + n for n in ("key", "em", "cl", "pl", "q", "emb", "w", "th")]
              + ["a%s%d_%d" % (k, c, t) for k in "pq" for c in range(NC) for t in range(1, STEPS + 1)])


def plan(ops):
    n = len(ops)
    rng = np.random.RandomState(P["seed"])
    succ = [[] for _ in range(n)]
    for o in ops:
        for d in o["deps"] | o["order"]:
            succ[d].append(o["n"])
    prio = [0.0] * n
    for i in range(n - 1, -1, -1):
        o = ops[i]
        prio[i] = o["busy"] + o["lat"] + P["hop"] + max([prio[s] for s in succ[i]] + [0.0])
    prio = [p - P["stag"][o["c"]] for p, o in zip(prio, ops)]
    if P["noise"]:
        prio = [p + P["noise"] * float(r) for p, r in zip(prio, rng.standard_normal(n))]
    missing = [len(o["deps"] | o["order"]) for o in ops]
    ready = [0.0] * n
    free = {}
    start = [0.0] * n
    cand = [i for i in range(n) if missing[i] == 0]
    while cand:
        best, rows = None, []
        for i in cand:
            e = ops[i]["eng"]
            s = ready[i] if e == "NET" else max(free.get(e, 0.0), ready[i])
            rows.append((s, i, e))
            if best is None or s < best[0]:
                best = (s, i, e)
        lim = best[0] + min(P["look"], ops[best[1]]["busy"])
        s, i, e = max((r for r in rows if r[2] == best[2] and r[0] <= lim), key=lambda r: (prio[r[1]], -r[1]))
        o = ops[i]
        start[i] = s
        if e != "NET":
            free[e] = s + o["busy"]
        fin = s + o["busy"] + o["lat"]
        cand.remove(i)
        for j in succ[i]:
            missing[j] -= 1
            ready[j] = max(ready[j], fin + P["hop"] if i in ops[j]["deps"] else s)
            if missing[j] == 0:
                cand.append(j)
    return start, max(start[i] + ops[i]["busy"] + ops[i]["lat"] for i in range(n))


def build(g, core, T, topo):
    rank = T.rank_of(core)
    cores = T.cores
    N = len(cores)
    V, S, PE, Y = g.vector, g.scalar, g.tensor, g.sync
    CY, FIX = P["cy"], P["fix"]
    ops = []
    lastw, readers, banks = {}, {}, {}
    cur = [0]

    def op(eng, emit, reads=(), writes=(), bank=None, busy=0.1, lat=0.0, sem=None, val=0):
        i = len(ops)
        deps, order = set(), set()
        for k in tuple(reads) + tuple(writes):
            if k in lastw:
                deps.add(lastw[k])
        for k in writes:
            deps.update(readers.get(k, ()))
        if bank:
            h = banks.setdefault(bank, {})
            for e, j in h.items():
                (order if e == eng else deps).add(j)
            h[eng] = i
        for k in reads:
            readers.setdefault(k, set()).add(i)
        for k in writes:
            lastw[k] = i
            readers[k] = set()
        ops.append({"n": i, "eng": eng, "emit": emit, "deps": deps, "order": order - deps, "busy": busy, "lat": lat, "sem": sem, "val": val, "c": cur[0]})
        return i

    def vd(cyc):
        return max(64, cyc) * CY + FIX

    def vts(out, in0, s1, s2, op0, op1, reads, writes, cyc=64, bank=None):
        if op1 is None:
            op("V", lambda: V.tensor_scalar(out, in0, s1, None, op0), reads, writes, bank, vd(cyc))
        else:
            op("V", lambda: V.tensor_scalar(out, in0, s1, s2, op0, op1), reads, writes, bank, vd(cyc))

    def vtt(out, in0, in1, o, reads, writes, cyc=64, bank=None):
        op("V", lambda: V.tensor_tensor(out, in0, in1, o), reads, writes, bank, vd(cyc))

    def vcp(out, in_, reads, writes, cyc=64, bank=None):
        op("V", lambda: V.tensor_copy(out, in_), reads, writes, bank, vd(cyc))

    def vfill(ap, x, reads, writes, cyc=64):
        op("V", lambda: V.memset(ap, x), reads, writes, None, vd(cyc))

    def scan(out, d0, d1, o0, o1, reads, writes, cyc=64, bank=None):
        op("V", lambda: V.tensor_tensor_scan(out, d0, d1, 0.0, o0, o1), reads, writes, bank, vd(cyc))

    def sact(out, in_, f, reads, writes, bank=None, cyc=64, **kw):
        op("S", lambda: S.activation(out, in_, f, **kw), reads, writes, bank, cyc * CY + 0.04)

    def gc(fn, writes, reads=(), busy=0.45):
        op("G", fn, reads, writes, None, busy)

    def mms(lst, reads, bank):
        def emit():
            r = None
            for (o, l, x, a, b) in lst:
                r = PE.matmul(o, l, x, a, b)
            return r
        op("P", emit, reads, (), bank, len(lst) * 64 * P["pe"] + 0.05)

    def load(q, out, in_, name, key, lat):
        op(q, lambda: (Y if q == "Y" else S).dma_start(out, in_), (), (key,), None, 0.1, lat, "ld_" + name, 16)

    load("Y", T.pl_s[:], T.pl[:], "pl", "pl_s", 2.0)
    load("S", T.qin[:, 0:192], T.q[:], "q", "q0", 2.2)
    load("Y", T.key_s[:], T.key[:], "key", "key", 5.0)
    load("S", T.w_s[:], T.w[:], "w", "w", 2.5)
    load("S", T.th_s[:], T.th[:], "th", "th", 2.5)
    load("S", T.emb_s[:], T.emb[:], "emb", "emb", 2.5)
    load("Y", T.cl_s[:], T.cl[:], "cl", "cl", 8.0)
    load("Y", T.em_s[:], T.em[:], "em", "em", 10.5)

    one64 = T.ones[:, 0:64]
    vfill(T.ones[:], 1.0, (), ("ones",))
    gc(lambda: g.iota(T.icol[:], [[0, 1]], 0, 1), ("icol",), (), 0.2)
    gc(lambda: g.affine_select(T.bd[:], T.ones[:], [[-16, 8], [0, 16]], A.is_ge, 0.0, 0, 1), ("bd",), ("ones",))
    gc(lambda: g.affine_select(T.bd[:], T.bd[:], [[16, 8], [0, 16]], A.is_ge, 0.0, 15, -1), ("bd",))
    gc(lambda: g.iota(T.rowl[:], [[1, 64]], 0, 0), ("rowl",), (), 0.3)
    gc(lambda: g.affine_select(T.idm[:], T.ones[:], [[-1, 128]], A.is_equal, 0.0, 0, 1), ("idm",), ("ones",))
    gc(lambda: g.affine_select(T.ltm[:], T.bd[:], [[1, 128]], A.is_gt, 0.0, 0, -1), ("ltm",), ("bd",))
    gc(lambda: g.iota(T.rowm[:], [[0, 4], [1, 16]], 0, 0, allow_small_or_imprecise_dtypes=True), ("rowm",), (), 0.3)
    vfill(T.wk[:], 0.0, (), ("wk0",), 1024)
    vfill(T.w2[:], 0.0, (), ("w20",), 1024)
    for c in range(NC):
        vcp(T.pin[:, 64 * c:64 * c + 64], T.pl_s[:, 64 * c:64 * c + 64], ("pl_s",), ("p%d_0" % c,))
    vts(T.kint[:], T.icol[:], 15, None, A.bitwise_and, None, ("icol",), ("kint",))
    vcp(T.kcol[:], T.kint[:], ("kint",), ("kcol",))
    vcp(T.rep[:], T.rowl[:], ("rowl",), ("rep",))
    r8 = range(8)
    wkk, w2k, ebk = tuple("wk%d" % b for b in r8), tuple("w2_%d" % b for b in r8), tuple("eb%d" % b for b in r8)
    for b in r8:
        sl = slice(16 * b, 16 * b + 129 * 15 + 1, 129)
        sact(T.wk[:, sl], T.bd[:, 16 * b:16 * b + 16], F.Copy, ("bd", "wk0"), (wkk[b],), scale=-1.0)
        vts(T.w2[:, sl], T.bd[:, 16 * b:16 * b + 16], 2.0, None, A.mult, None, ("bd", "w20"), (w2k[b],))
    sact(T.nbd[:], T.bd[:], F.Copy, ("bd",), ("nbd",), None, 128, scale=-1.0)
    vts(T.bdw[:], T.bd[:], T.w_s[:, 0:1], None, A.mult, None, ("bd", "w"), ("bdw",))
    vcp(T.idh[:], T.idm[:], ("idm",), ("idh",))
    vts(T.c1023[:], one64, -1023.5, None, A.mult, None, ("ones",), ("c1023",))
    vfill(T.cb[:], -524288.0, (), ("cb",))
    sact(T.in2k[:], T.idm[:], F.Copy, ("idm",), ("in2k",), None, 128, scale=-2048.0)
    sact(T.i8k[:], T.idm[:], F.Copy, ("idm",), ("i8k",), None, 128, scale=8192.0)
    sact(T.bd4k[:], T.bd[:], F.Copy, ("bd",), ("bd4k",), None, 128, scale=4096.0)
    vts(T.mb2[:], T.rowm[:], T.kcol[:, 0:1], -8192.0, A.is_equal, A.mult, ("rowm", "kcol"), ("mb2",))
    vts(T.mb[:], T.mb2[:], 4096.0, None, A.add, None, ("mb2",), ("mb",))
    vtt(T.gw0[:], T.idm[:], T.ltm[:], A.subtract, ("idm", "ltm"), ("gw0",), 256)
    sact(T.gw[:], T.gw0[:], F.Copy, ("gw0",), ("gw",), None, 128, scale=4096.0)
    vts(T.sgcol[:], T.kcol[:], -4096.0, 57344.0, A.mult, A.add, ("kcol",), ("sgcol",))
    vts(T.sg[:], T.bd[:], T.sgcol[:, 0:1], None, A.mult, None, ("bd", "sgcol"), ("sg",))
    vcp(T.bdh[:], T.bd[:], ("bd",), ("bdh",))
    vfill(T.rst32[:], 1.0, (), ("rst32",), 128)
    vfill(T.rst32[:, 0:128:32], 0.0, (), ("rst32",))
    sact(T.i16[:], T.idm[:], F.Copy, ("idm",), ("i16",), None, 128, scale=16.0)
    vts(T.ck[:], one64, T.kcol[:, 0:1], -1.0, A.mult, A.mult, ("ones", "kcol"), ("ck",))
    vts(T.gint[:], T.icol[:], 4, 1, A.logical_shift_right, A.bitwise_and, ("icol",), ("gint",))
    vts(T.gcol[:], T.gint[:], 65536.0, None, A.mult, None, ("gint",), ("gcol",))
    vfill(T.rowb[:, 0:32], 0.0, (), ("rowb0",))
    vfill(T.rowb[:, 32:64], 131072.0, (), ("rowb1",))
    vts(T.ckb[:], T.rowb[:], T.gcol[:, 0:1], None, A.add, None, ("rowb0", "rowb1", "gcol"), ("ckb",))
    vfill(T.zero[:], 0.0, (), ("zero",))
    vfill(T.big16[:], 0.0, (), ("big16",))
    vfill(T.big16[:, 0:64:16], 8388608.0, (), ("big16",))
    for c in range(NC):
        vfill(T["vs%d" % c][:, 64:80], 4194304.0, (), ("vsp%d" % c,))
    sact(T.ihf[:], T.idm[:], F.Copy, ("idm",), ("ihf",), None, 128, scale=0.5)
    vfill(T.cq[:], -0.25, (), ("cq",))
    vcp(T.bdc[:], T.bd[:, 0:128:16], ("bd",), ("bdc",))
    vts(T.tw[:], T.bdc[:], T.kcol[:, 0:1], None, A.mult, None, ("bdc", "kcol"), ("tw",))
    for b in r8:
        vts(T.eb[:, 16 * b:16 * b + 16], T.emb_s[:], T.bdc[:, b:b + 1], 0.5, A.mult, A.mult, ("emb", "bdc"), (ebk[b],))

    def gather(e, out, win, off, reads, writes, count):
        fn = (lambda: S.activation(out, win.indirect(off), F.Copy)) if e == "S" else (lambda: V.tensor_copy(out, win.indirect(off)))
        op(e, fn, reads, writes, None, 0.07 + count * P["gather"] * CY)

    sends = [0]

    def send(dst, out, in_, sem, key, akey):
        eng = topo.engines(core, dst)[:8]
        rid, pid, _ = topo.addr(dst)
        m = sum(1 << x for x in eng)
        sends[0] += len(eng)
        i = op("G", lambda: g.remote_dma(out, in_, T.sem[sem], T.sem.lsem, pid, rid, m), (key,), (), None, 0.15)
        ops[i]["remote"] = True
        j = op("NET", None, (), (akey,), None, 0.0, P["net"], sem, len(eng))
        ops[j]["deps"].add(i)

    def step(t, c):
        cur[0] = c
        B = lambda n: T["%s%d" % (n, c)]
        k = lambda n: "%s%d" % (n, c)
        o0 = t * 192 + NL * c
        o1 = o0 + 192
        pin, qin = T.pin[:, o0:o0 + NL], T.qin[:, o0:o0 + NL]
        pkey = "p%d_%d" % (c, t)
        qkey = "q%d_%d" % (c, t) if t else "q0"
        psd, psx = B("psd"), B("psx")
        bd, bx = "D%d" % c, "X%d" % c
        kg, mx, eg = B("kg"), B("mx"), B("eg")
        D, U, AR = psd[:, 0:64], psd[:, 64:128], psd[:, 128:192]
        CH, C0, C1 = psx[:, 0:128], psx[:, 0:128:2], psx[:, 1:128:2]
        HA, VO, QO, TK, V2 = psx[:, 128:192], psx[:, 192:256], psx[:, 256:320], psx[0:8, 320:384], psx[:, 384:448]
        kgk, a = [], 0
        for e, w in P["K"]:
            kgk.append("%s_%d" % (k("kg"), a))
            gather(e, kg[:, 16 * a:16 * (a + w)], T.key_s[:], T.pin[:, o0 + a:o0 + a + w], ("key", pkey), (kgk[-1],), 16 * w)
            a += w
        kgk = tuple(kgk)
        vts(B("pc")[:], pin, 0.5, -0.25, A.mult, A.add, (pkey,), (k("pc"),))
        vts(B("ph")[:], pin, -2048.0, None, A.add, None, (pkey,), (k("ph"),))
        mms([(D, T.wk[:, 128 * i:128 * i + 128], kg[:, i:1024:16], i == 0, False) for i in range(NS)], kgk + wkk, bd)
        mms([(D, T.nbd[:], qin, False, False)], ("nbd", qkey), bd)
        mxk, a = [], 0
        for w in P["M"]:
            mxk.append("%s_%d" % (k("mx"), a))
            op("V", lambda s=slice(16 * a, 16 * (a + w)), a=a, w=w: V.tensor_tensor(mx[:, s], qin.indirect(T.rep[:, a:a + w]), kg[:, s], A.max),
               ("rep", qkey) + kgk, (mxk[-1],), None, 0.06 + 16 * w * P["gather"] * CY)
            a += w
        mms([(HA, T.bdw[:], qin, True, False), (HA, T.idh[:], T.c1023[:], False, False), (HA, T.idm[:], T.cb[:], False, True)],
            ("bdw", "idh", "c1023", "idm", "cb", qkey), bx)
        sact(B("hy")[:], HA, F.Identity, (), (k("hy"),), bx, bias=BIG, scale=1.0 / 2048.0)
        sact(B("hn")[:], B("hy")[:], F.Identity, (k("hy"),), (k("hn"),), bias=-BIG)
        mms([(C1, T.bdw[:], qin, True, False), (C1, T.idm[:], T.mb2[:], False, False), (C1, T.idm[:], T.cb[:], False, False),
             (C1, T.in2k[:], B("hn")[:], False, False)], ("in2k", "mb2", k("hn")), bx)
        mms([(D, T.w2[:, 128 * i:128 * i + 128], mx[:, i:1024:16], False, i == NS - 1) for i in range(NS)], tuple(mxk) + w2k, bd)
        vts(B("nr")[:], D, T.th_s[:, 0:1], None, A.is_lt, None, ("th",), (k("nr"),), 64, bd)
        mms([(U, T.gw[:], B("nr")[:], True, True)], ("gw", k("nr")), bd)
        mms([(C1, T.bd4k[:], B("nr")[:], False, True), (C0, T.idm[:], T.mb[:], True, False), (C0, T.sg[:], B("nr")[:], False, False)],
            ("bd4k", "idm", "mb", "sg", k("nr")), bx)
        mms([(AR, T.idh[:], B("ph")[:], True, False), (AR, T.i8k[:], B("nr")[:], False, True)], ("idh", "i8k", k("nr"), k("ph")), bd)
        vtt(B("xx")[:], U, B("pc")[:], A.min, (k("pc"),), (k("xx"),), 64, bd)
        sact(B("ar")[:], AR, F.Identity, (), (k("ar"),), bd, bias=-2048.0)
        mms([(C0, T.bdh[:], B("xx")[:], False, True)], ("bdh", k("xx")), bx)
        scan(B("sc")[:], T.rst32[:], CH, A.mult, A.min, ("rst32",), (k("sc"),), 128, bx)
        vts(B("ci")[:], B("sc")[:, 31:128:32], 8192.0, None, A.add, None, (k("sc"),), (k("ci"),))
        op("V", lambda: V.tensor_tensor(B("pf")[:], T.cl_s[:].indirect(B("ci")[:, 0:4]), B("ar")[:], A.max),
           ("cl", k("ci"), k("ar")), (k("pf"),), None, 0.06 + 64 * P["gather"] * CY)
        vts(B("s2")[:], B("pf")[:], PL - 1, None, A.bitwise_and, None, (k("pf"),), (k("s2"),))
        pok = "po%d_%d" % (c, t)
        vcp(T.pout[:, o0:o0 + NL], B("s2")[:], (k("s2"),), (pok,))
        nxt = cores[(rank + 1) % N if c == 0 else (rank - 1) % N]
        shift = 1 if (c == 0 and rank == N - 1) else (PL - 1 if (c and rank == 0) else 0)
        src, sk = T.pout[:, o0:o0 + NL], pok
        if shift:
            src, sk = T.pw[:, o0:o0 + NL], "pw%d_%d" % (c, t)
            vts(B("s1")[:], B("pf")[:], float(shift), None, A.add, None, (k("pf"),), (k("s1"),))
            vts(B("s3")[:], B("s1")[:], PL - 1, None, A.bitwise_and, None, (k("s1"),), (k("s3"),))
            vcp(src, B("s3")[:], (k("s3"),), (sk,))
        send(nxt, T.pin[:, o1:o1 + NL], src, "ap%d_%d" % (c, t + 1), sk, "p%d_%d" % (c, t + 1))
        egk, a = [], 0
        for e, w in P["E"]:
            egk.append("%s_%d" % (k("eg"), a))
            gather(e, eg[:, 16 * a:16 * (a + w)], T.em_s[:], T.pout[:, o0 + a:o0 + a + w], ("em", pok), (egk[-1],), 16 * w)
            a += w
        mms([(VO, T.idm[:], T.ck[:], True, False), (VO, T.idm[:], T.ckb[:], False, False)], ("idm", "ck", "ckb"), bx)
        mms([(VO, T.i16[:], eg[:, i:1024:16], False, i == NS - 1) for i in range(NS)], tuple(egk) + ("i16",), bx)
        op("V", lambda: V.transpose(B("vt")[:], VO), (), (k("vt"),), bx, vd(64))
        mms([(QO, T.idm[:], T.cq[:], True, False), (QO, T.ihf[:], qin, False, False)], ("idm", "cq", "ihf", qkey), bx)
        scan(B("vs")[:, 0:64], T.zero[:], B("vt")[:], A.max, A.max, ("zero", k("vt")), (k("vs"),))
        scan(V2, T.big16[:], B("vs")[:, 15:79], A.max, A.min, ("big16", k("vs"), k("vsp")), (k("v2"),), 64, bx)
        vtt(B("oh")[:], B("vt")[:], V2, A.is_equal, (k("vt"), k("v2")), (k("oh"),), 64, bx)
        op("V", lambda: V.transpose(B("ot")[:], B("oh")[:]), (k("oh"),), (k("ot"),), None, vd(64))
        mms([(QO, T.eb[:], B("ot")[:], False, True)], ebk + (k("ot"),), bx)
        mms([(TK, T.tw[:], B("ot")[:], True, True)], ("tw", k("ot")), bx)
        qok = "qo%d_%d" % (c, t)
        vts(T.qout[:, o0:o0 + NL], QO, BIG, BIG, A.add, A.subtract, (), (qok,), 64, bx)
        sact(T.yt_s[0:8, o0:o0 + NL], TK, F.Copy, (), ("yt%d_%d" % (c, t),), bx)
        send(nxt, T.qin[:, o1:o1 + NL], T.qout[:, o0:o0 + NL], "aq%d_%d" % (c, t + 1), qok, "q%d_%d" % (c, t + 1))

    for t in range(STEPS):
        for c in range(NC):
            step(t, c)
    nout = [0]

    def store(out, in_, reads):
        nout[0] += 16
        op("Y", lambda: Y.dma_start(out, in_), reads, (), None, 0.1, 2.0, "outs", None)

    o6 = STEPS * 192
    for c in range(NC):
        a, b = NL * c, NL * c + NL
        vcp(T.yp_s[:, a:b], T.pin[:, o6 + a:o6 + b], ("p%d_%d" % (c, STEPS),), ("yp%d" % c,))
        store(T.yp[:, a:b], T.yp_s[:, a:b], ("yp%d" % c,))
        store(T.yq[:, a:b], T.qin[:, o6 + a:o6 + b], ("q%d_%d" % (c, STEPS),))
    store(T.yt[:], T.yt_s[0:8, :], tuple("yt%d_%d" % (c, t) for c in range(NC) for t in range(STEPS)))
    return ops, sends[0], nout[0]


def emit_all(g, T, ops, start, nsend, nout):
    eng = {"V": g.vector, "S": g.scalar, "P": g.tensor, "G": g, "Y": g.sync}
    esem = {"V": "sV", "S": "sS", "P": "sP", "G": "sG"}
    count = {e: 0 for e in eng}
    known = {e: {} for e in eng}
    fin = {}
    for i in sorted(range(len(ops)), key=lambda x: (start[x], x)):
        o = ops[i]
        e = o["eng"]
        if e == "NET":
            fin[i] = (o["sem"], o["val"], {o["sem"]: o["val"]})
            continue
        kn = known[e]
        need = {}
        for d in o["deps"]:
            s, v, _ = fin[d]
            if kn.get(s, 0) < v and need.get(s, (0, None))[0] < v:
                need[s] = (v, d)
        for s in list(need):
            v = need[s][0]
            if any(s2 != s and fin[need[s2][1]][2].get(s, 0) >= v for s2 in need):
                del need[s]
        for s in sorted(need):
            v, d = need[s]
            eng[e].wait_ge(T.sem[s], v)
            for s2, v2 in fin[d][2].items():
                if kn.get(s2, 0) < v2:
                    kn[s2] = v2
        ins = o["emit"]()
        c = dict(kn)
        if o["sem"] is not None:
            ins.then_inc(T.sem[o["sem"]], 16)
            if o["val"]:
                c[o["sem"]] = o["val"]
            fin[i] = (o["sem"], o["val"], c)
        elif not o.get("remote"):
            count[e] += 1
            ins.then_inc(T.sem[esem[e]], 1)
            c[esem[e]] = count[e]
            fin[i] = (esem[e], count[e], c)
    g.wait_ge(T.sem.lsem, nsend)
    for e in ("V", "S", "P", "G"):
        g.wait_ge(T.sem[esem[e]], count[e])
    g.sync.wait_ge(T.sem.outs, nout)


def rank_program(g, core, T, topo):
    if T.rank_of(core) is None:
        return
    ops, nsend, nout = build(g, core, T, topo)
    start, _ = plan(ops)
    emit_all(g, T, ops, start, nsend, nout)
